import numpy as np, ml_dtypes
CORES = [6,14,22,30,38,134,142,150,158]
N = 9
F = 256
GROUPS = [[0,3,6],[1,4,7],[2,5,8]]
def setup_inputs(rng):
    return {"x": rng.standard_normal((N, 128, F), dtype=np.float32).astype(ml_dtypes.bfloat16), "w": (rng.standard_normal((N, 128, 128), dtype=np.float32) / 11).astype(ml_dtypes.bfloat16)}
def setup_inputs_big(rng):
    d = setup_inputs(rng)
    for k in ("x", "w"): d[k] = (d[k].astype(np.float32) * 1024.0).astype(d[k].dtype)
    return d
def setup_inputs_small(rng):
    d = setup_inputs(rng)
    for k in ("x", "w"): d[k] = (d[k].astype(np.float32) * (1 / 1024.0)).astype(d[k].dtype)
    return d
def setup_inputs_apart(rng):
    d = setup_inputs(rng)
    f = (10.0 ** rng.permutation(np.linspace(-1.5, 1.5, N))).astype(np.float32).reshape(N, 1, 1)
    for k in ("x", "w"): d[k] = (d[k].astype(np.float32) * f).astype(d[k].dtype)
    return d
def reference(x, w):
    X, W = x.astype(np.float64), w.astype(np.float64)
    s = sum(W[g[0]].T @ np.maximum(sum(X[j] for j in g), 0.0) for g in GROUPS).astype(ml_dtypes.bfloat16)
    return {"y": np.broadcast_to(s, (N,) + s.shape)}

@@ -1,0 +1,164 @@
+from concourse.bass import DstId, RemoteDMATransfer
+from concourse.mybir import AluOpType
+
+F = 256
+K = 128
+WORLD = 256
+
+SCRATCH = {
+    "in0": ("sbuf", [128, F + K], "bfloat16"),
+    "in1": ("sbuf", [128, F], "bfloat16"),
+    "in2": ("sbuf", [128, F], "bfloat16"),
+    "zero": ("sbuf", [128, F], "bfloat16"),
+    "t": ("sbuf", [128, F], "bfloat16"),
+    "q0": ("sbuf", [128, F], "bfloat16"),
+    "q1": ("sbuf", [128, F], "bfloat16"),
+    "q2": ("sbuf", [128, F], "bfloat16"),
+    "yb": ("sbuf", [128, F], "bfloat16"),
+    "ps": ("psum", [128, 512], "float32"),
+    "pp": ("psum", [128, 512], "float32"),
+}
+SEMAPHORES = ["ldx", "ldw", "arr0", "arr1", "arr2", "zs", "v1", "v2", "v3", "mm", "cp",
+              "par0", "par1", "par2", "v4", "v5", "st", "sent"]
+
+
+def _place(topo, c):
+    return (topo.host(c), topo.chip(c))
+
+
+def _links(topo, a, b):
+    if _place(topo, a) == _place(topo, b):
+        return []
+    d = topo.die(a)
+    if topo.mates(a, b):
+        return [("mate", _place(topo, a), d)]
+    if topo.same_plane(a, b):
+        return [("out", _place(topo, a), d), ("in", _place(topo, b), d)]
+    m = [c for c in range(WORLD) if topo.mates(a, c)][0]
+    return [("mate", _place(topo, a), d), ("out", _place(topo, m), d), ("in", _place(topo, b), d)]
+
+
+def _splits(items):
+    out = []
+    n = len(items)
+    for a in range(n):
+        for b in range(a + 1, n):
+            rest = [items[k] for k in range(n) if k != a and k != b]
+            for c in range(1, len(rest)):
+                last = [rest[k] for k in range(1, len(rest)) if k != c]
+                for pair2, pair3 in (([rest[0], rest[c]], last), (last, [rest[0], rest[c]])):
+                    out.append([items[a], items[b]] + pair2 + pair3)
+    return out
+
+
+def _round2_plan(topo, cores, groups):
+    load, plan = {}, {}
+    for grp in groups:
+        outs = [r for r in range(len(cores)) if r not in grp]
+        best = None
+        for p in _splits(outs):
+            l = dict(load)
+            for k, r in enumerate(p):
+                for key in _links(topo, cores[grp[k // 2]], cores[r]):
+                    l[key] = l.get(key, 0) + 1
+            score = sum(v * v for v in l.values())
+            if best is None or score < best[0]:
+                best = (score, p, l)
+        load = best[2]
+        for k, r in enumerate(best[1]):
+            plan.setdefault(grp[k // 2], []).append(r)
+    return plan
+
+
+def _mask(topo, src, dsts):
+    m = topo.mask(src, dsts[0])
+    for d in dsts[1:]:
+        m &= topo.mask(src, d)
+    return m
+
+
+def _engines(mask):
+    return bin(mask).count("1")
+
+
+def _send(g, topo, core, dsts, ap, remote_sem, local_sem):
+    mask = _mask(topo, core, dsts)
+    ids = []
+    for d in dsts:
+        rid, pid = topo.addr(d, core)
+        ids.append(DstId(rid=rid, pnc=pid))
+    g.remote_dma_fused([RemoteDMATransfer(dst_ids=ids, dma_engine_mask=mask, remote_sem=remote_sem,
+                                          srcs=[ap], dsts=[ap for _ in dsts], alu_op=0)], local_sem=local_sem)
+    return _engines(mask)
+
+
+def rank_program(g, core, T, topo):
+    rank = T.rank_of(core)
+    if rank is None:
+        return
+    groups, cores, S = T.tables["GROUPS"], T.cores, T.sem
+    gi = [k for k, grp in enumerate(groups) if rank in grp][0]
+    grp = groups[gi]
+    mi = grp.index(rank)
+    first = mi == 0
+    plan = _round2_plan(topo, cores, groups)
+
+    xs = [T.in0[:, 0:F], T.in1[:, :], T.in2[:, :]]
+    wg = T.in0[:, F:F + K]
+    whole = [T.in0[:, :], T.in1[:, :], T.in2[:, :]]
+    q = [T.q0[:, :], T.q1[:, :], T.q2[:, :]]
+    arr = [S.arr0, S.arr1, S.arr2]
+    par = [S.par0, S.par1, S.par2]
+    s_a, s_b, p = T.ps[:, 0:F], T.ps[:, F:2 * F], T.pp[:, 0:F]
+
+    g.sync.dma_start(xs[mi], T.x[:, :]).then_inc(S.ldx, 16)
+    if first:
+        g.scalar.dma_start(wg, T.w[:, :]).then_inc(S.ldw, 16)
+    g.vector.memset(T.zero[:, :], 0.0).then_inc(S.zs, 1)
+
+    peers = [m for m in range(len(grp)) if m != mi]
+    g.wait_ge(S.ldx, 16)
+    if first:
+        g.wait_ge(S.ldw, 16)
+    sent = _send(g, topo, core, [cores[grp[m]] for m in peers], whole[mi], arr[mi], S.sent)
+
+    def arrived1(m):
+        return _engines(_mask(topo, cores[grp[m]], [cores[grp[o]] for o in range(len(grp)) if o != m]))
+
+    late, early = peers[0], peers[1]
+    v, te = g.vector, g.tensor
+    v.wait_ge(S.ldx, 16)
+    v.wait_ge(arr[early], arrived1(early))
+    v.tensor_tensor(s_a, xs[mi], xs[early], AluOpType.add).then_inc(S.v1, 1)
+    v.wait_ge(arr[late], arrived1(late))
+    v.wait_ge(S.v1, 1)
+    v.tensor_tensor(s_b, s_a, xs[late], AluOpType.add).then_inc(S.v2, 1)
+    v.wait_ge(S.zs, 1)
+    v.wait_ge(S.v2, 1)
+    v.tensor_tensor(T.t[:, :], s_b, T.zero[:, :], AluOpType.max).then_inc(S.v3, 1)
+    if first:
+        te.wait_ge(S.ldw, 16)
+    else:
+        te.wait_ge(arr[0], arrived1(0))
+    te.wait_ge(S.v3, 1)
+    te.matmul(p, wg, T.t[:, :], True, True).then_inc(S.mm, 1)
+    v.wait_ge(S.mm, 1)
+    v.tensor_copy(q[gi], p).then_inc(S.cp, 1)
+
+    g.wait_ge(S.cp, 1)
+    sent += _send(g, topo, core, [cores[r] for r in plan[rank]], q[gi], par[gi], S.sent)
+
+    def arrived2(k):
+        src = [r for r in groups[k] if rank in plan[r]][0]
+        return _engines(_mask(topo, cores[src], [cores[r] for r in plan[src]]))
+
+    ga, gb = [k for k in range(len(groups)) if k != gi]
+    v.wait_ge(par[ga], arrived2(ga))
+    v.tensor_tensor(s_a, p, q[ga], AluOpType.add).then_inc(S.v4, 1)
+    v.wait_ge(par[gb], arrived2(gb))
+    v.wait_ge(S.v4, 1)
+    v.tensor_tensor(T.yb[:, :], s_a, q[gb], AluOpType.add).then_inc(S.v5, 1)
+    g.sync.wait_ge(S.v5, 1)
+    g.sync.dma_start(T.y[:, :], T.yb[:, :]).then_inc(S.st, 16)
+    g.sync.wait_ge(S.st, 16)
+    g.wait_ge(S.sent, sent)

@@ -4,22 +4,28 @@ from concourse.mybir import AluOpType
 F = 256
 K = 128
 WORLD = 256
+NB = 2
+H = F // NB
 
 SCRATCH = {
     "in0": ("sbuf", [128, F + K], "bfloat16"),
     "in1": ("sbuf", [128, F], "bfloat16"),
     "in2": ("sbuf", [128, F], "bfloat16"),
+    "e": ("sbuf", [128, K + 1], "bfloat16"),
+    "ed": ("dram", [K + 1, 128], "bfloat16"),
+    "idn": ("sbuf", [128, K], "bfloat16"),
     "zero": ("sbuf", [128, F], "bfloat16"),
     "t": ("sbuf", [128, F], "bfloat16"),
     "q0": ("sbuf", [128, F], "bfloat16"),
     "q1": ("sbuf", [128, F], "bfloat16"),
     "q2": ("sbuf", [128, F], "bfloat16"),
     "yb": ("sbuf", [128, F], "bfloat16"),
-    "ps": ("psum", [128, 512], "float32"),
-    "pp": ("psum", [128, 512], "float32"),
 }
-SEMAPHORES = ["ldx", "ldw", "arr0", "arr1", "arr2", "zs", "v1", "v2", "v3", "mm", "cp",
-              "par0", "par1", "par2", "v4", "v5", "st", "sent"]
+SEMAPHORES = ["ldx", "ldw", "arr0", "arr1", "arr2", "par0", "par1", "par2", "zs", "e1", "e2", "ew", "er", "st", "sent"]
+for _h in range(NB):
+    SCRATCH["sb%d" % _h] = ("psum", [128, 512], "float32")
+    SCRATCH["pp%d" % _h] = ("psum", [128, 512], "float32")
+    SEMAPHORES += [n + str(_h) for n in ("s_", "r_", "mm_", "cp_", "fa_", "f2_")]
 
 
 def _place(topo, c):
@@ -102,19 +108,34 @@ def rank_program(g, core, T, topo):
     mi = grp.index(rank)
     first = mi == 0
     plan = _round2_plan(topo, cores, groups)
+    v, te = g.vector, g.tensor
+    blocks = range(NB)
 
-    xs = [T.in0[:, 0:F], T.in1[:, :], T.in2[:, :]]
+    def blk(t, h):
+        return t[:, h * H:(h + 1) * H]
+
+    xin = [T.in0, T.in1, T.in2]
     wg = T.in0[:, F:F + K]
     whole = [T.in0[:, :], T.in1[:, :], T.in2[:, :]]
-    q = [T.q0[:, :], T.q1[:, :], T.q2[:, :]]
+    q = [T.q0, T.q1, T.q2]
     arr = [S.arr0, S.arr1, S.arr2]
     par = [S.par0, S.par1, S.par2]
-    s_a, s_b, p = T.ps[:, 0:F], T.ps[:, F:2 * F], T.pp[:, 0:F]
+    sb = [T["sb%d" % h][:, 0:H] for h in blocks]
+    pp = [T["pp%d" % h][:, 0:H] for h in blocks]
+    idn = T.idn[:, :]
 
-    g.sync.dma_start(xs[mi], T.x[:, :]).then_inc(S.ldx, 16)
+    g.sync.dma_start(xin[mi][:, 0:F], T.x[:, :]).then_inc(S.ldx, 16)
     if first:
         g.scalar.dma_start(wg, T.w[:, :]).then_inc(S.ldw, 16)
-    g.vector.memset(T.zero[:, :], 0.0).then_inc(S.zs, 1)
+
+    v.memset(T.e[:, :], 0.0).then_inc(S.e1, 1)
+    v.wait_ge(S.e1, 1)
+    v.memset(T.e[:, 0:1], 1.0).then_inc(S.e2, 1)
+    v.memset(T.zero[:, :], 0.0).then_inc(S.zs, 1)
+    g.scalar.wait_ge(S.e2, 1)
+    g.scalar.dma_start(T.ed[:, :], T.e[:, :]).then_inc(S.ew, 16)
+    g.scalar.wait_ge(S.ew, 16)
+    g.scalar.dma_start(idn, T.ed[0:128, :]).then_inc(S.er, 16)
 
     peers = [m for m in range(len(grp)) if m != mi]
     g.wait_ge(S.ldx, 16)
@@ -126,39 +147,49 @@ def rank_program(g, core, T, topo):
         return _engines(_mask(topo, cores[grp[m]], [cores[grp[o]] for o in range(len(grp)) if o != m]))
 
     late, early = peers[0], peers[1]
-    v, te = g.vector, g.tensor
-    v.wait_ge(S.ldx, 16)
-    v.wait_ge(arr[early], arrived1(early))
-    v.tensor_tensor(s_a, xs[mi], xs[early], AluOpType.add).then_inc(S.v1, 1)
-    v.wait_ge(arr[late], arrived1(late))
-    v.wait_ge(S.v1, 1)
-    v.tensor_tensor(s_b, s_a, xs[late], AluOpType.add).then_inc(S.v2, 1)
+    te.wait_ge(S.er, 16)
+    te.wait_ge(S.ldx, 16)
+    for h in blocks:
+        te.matmul(sb[h], idn, blk(xin[mi], h), True, False)
+    te.wait_ge(arr[early], arrived1(early))
+    for h in blocks:
+        te.matmul(sb[h], idn, blk(xin[early], h), False, False)
+    te.wait_ge(arr[late], arrived1(late))
+    for h in blocks:
+        te.matmul(sb[h], idn, blk(xin[late], h), False, True).then_inc(S["s_%d" % h], 1)
     v.wait_ge(S.zs, 1)
-    v.wait_ge(S.v2, 1)
-    v.tensor_tensor(T.t[:, :], s_b, T.zero[:, :], AluOpType.max).then_inc(S.v3, 1)
+    for h in blocks:
+        v.wait_ge(S["s_%d" % h], 1)
+        v.tensor_tensor(blk(T.t, h), sb[h], blk(T.zero, h), AluOpType.max).then_inc(S["r_%d" % h], 1)
     if first:
         te.wait_ge(S.ldw, 16)
-    else:
-        te.wait_ge(arr[0], arrived1(0))
-    te.wait_ge(S.v3, 1)
-    te.matmul(p, wg, T.t[:, :], True, True).then_inc(S.mm, 1)
-    v.wait_ge(S.mm, 1)
-    v.tensor_copy(q[gi], p).then_inc(S.cp, 1)
+    for h in blocks:
+        te.wait_ge(S["r_%d" % h], 1)
+        te.matmul(pp[h], wg, blk(T.t, h), True, True).then_inc(S["mm_%d" % h], 1)
+    for h in blocks:
+        v.wait_ge(S["mm_%d" % h], 1)
+        v.tensor_copy(blk(q[gi], h), pp[h]).then_inc(S["cp_%d" % h], 1)
+    for h in blocks:
+        te.matmul(sb[h], wg, blk(T.t, h), True, False)
 
-    g.wait_ge(S.cp, 1)
-    sent += _send(g, topo, core, [cores[r] for r in plan[rank]], q[gi], par[gi], S.sent)
+    for h in blocks:
+        g.wait_ge(S["cp_%d" % h], 1)
+    sent += _send(g, topo, core, [cores[r] for r in plan[rank]], q[gi][:, :], par[gi], S.sent)
 
     def arrived2(k):
         src = [r for r in groups[k] if rank in plan[r]][0]
         return _engines(_mask(topo, cores[src], [cores[r] for r in plan[src]]))
 
     ga, gb = [k for k in range(len(groups)) if k != gi]
-    v.wait_ge(par[ga], arrived2(ga))
-    v.tensor_tensor(s_a, p, q[ga], AluOpType.add).then_inc(S.v4, 1)
+    te.wait_ge(par[ga], arrived2(ga))
+    for h in blocks:
+        te.matmul(sb[h], idn, blk(q[ga], h), False, True).then_inc(S["fa_%d" % h], 1)
     v.wait_ge(par[gb], arrived2(gb))
-    v.wait_ge(S.v4, 1)
-    v.tensor_tensor(T.yb[:, :], s_a, q[gb], AluOpType.add).then_inc(S.v5, 1)
-    g.sync.wait_ge(S.v5, 1)
+    for h in blocks:
+        v.wait_ge(S["fa_%d" % h], 1)
+        v.tensor_tensor(blk(T.yb, h), sb[h], blk(q[gb], h), AluOpType.add).then_inc(S["f2_%d" % h], 1)
+    for h in blocks:
+        g.sync.wait_ge(S["f2_%d" % h], 1)
     g.sync.dma_start(T.y[:, :], T.yb[:, :]).then_inc(S.st, 16)
     g.sync.wait_ge(S.st, 16)
     g.wait_ge(S.sent, sent)

@@ -4,11 +4,14 @@ from concourse.mybir import AluOpType
 F = 256
 K = 128
 WORLD = 256
-NB = 2
-H = F // NB
+RB = 2
+BW = F // RB
+SB = 2
+H = BW // SB
+NS = RB * SB
 
 SCRATCH = {
-    "in0": ("sbuf", [128, F + K], "bfloat16"),
+    "in0": ("sbuf", [128, K + F], "bfloat16"),
     "in1": ("sbuf", [128, F], "bfloat16"),
     "in2": ("sbuf", [128, F], "bfloat16"),
     "e": ("sbuf", [128, K + 1], "bfloat16"),
@@ -21,8 +24,10 @@ SCRATCH = {
     "q2": ("sbuf", [128, F], "bfloat16"),
     "yb": ("sbuf", [128, F], "bfloat16"),
 }
-SEMAPHORES = ["ldx", "ldw", "arr0", "arr1", "arr2", "par0", "par1", "par2", "zs", "e1", "e2", "ew", "er", "st", "sent"]
-for _h in range(NB):
+SEMAPHORES = ["ldw", "zs", "e1", "e2", "ew", "er", "sent"]
+for _b in range(RB):
+    SEMAPHORES += ["st%d" % _b, "ldx%d" % _b] + ["arr%d_%d" % (_m, _b) for _m in range(3)] + ["par%d_%d" % (_m, _b) for _m in range(3)]
+for _h in range(NS):
     SCRATCH["sb%d" % _h] = ("psum", [128, 512], "float32")
     SCRATCH["pp%d" % _h] = ("psum", [128, 512], "float32")
     SEMAPHORES += [n + str(_h) for n in ("s_", "r_", "mm_", "cp_", "fa_", "f2_")]
@@ -109,22 +114,37 @@ def rank_program(g, core, T, topo):
     first = mi == 0
     plan = _round2_plan(topo, cores, groups)
     v, te = g.vector, g.tensor
-    blocks = range(NB)
+    blocks = range(RB)
 
-    def blk(t, h):
+    def subs(b):
+        return range(b * SB, (b + 1) * SB)
+
+    def sub(t, h):
         return t[:, h * H:(h + 1) * H]
 
-    xin = [T.in0, T.in1, T.in2]
-    wg = T.in0[:, F:F + K]
-    whole = [T.in0[:, :], T.in1[:, :], T.in2[:, :]]
+    def blk(t, b):
+        return t[:, b * BW:(b + 1) * BW]
+
+    slot = [T.in0, T.in1, T.in2]
+    off = [K, 0, 0]
+
+    def xs(m, h):
+        return slot[m][:, off[m] + h * H:off[m] + (h + 1) * H]
+
+    def piece(m, b):
+        lo = 0 if b == 0 else off[m] + b * BW
+        return slot[m][:, lo:off[m] + (b + 1) * BW]
+
+    wg = T.in0[:, 0:K]
     q = [T.q0, T.q1, T.q2]
-    arr = [S.arr0, S.arr1, S.arr2]
-    par = [S.par0, S.par1, S.par2]
-    sb = [T["sb%d" % h][:, 0:H] for h in blocks]
-    pp = [T["pp%d" % h][:, 0:H] for h in blocks]
+    arr = [[S["arr%d_%d" % (m, b)] for b in blocks] for m in range(3)]
+    par = [[S["par%d_%d" % (k, b)] for b in blocks] for k in range(3)]
+    sb = [T["sb%d" % h][:, 0:H] for h in range(NS)]
+    pp = [T["pp%d" % h][:, 0:H] for h in range(NS)]
     idn = T.idn[:, :]
 
-    g.sync.dma_start(xin[mi][:, 0:F], T.x[:, :]).then_inc(S.ldx, 16)
+    for b in blocks:
+        g.sync.dma_start(slot[mi][:, off[mi] + b * BW:off[mi] + (b + 1) * BW], blk(T.x, b)).then_inc(S["ldx%d" % b], 16)
     if first:
         g.scalar.dma_start(wg, T.w[:, :]).then_inc(S.ldw, 16)
 
@@ -138,58 +158,71 @@ def rank_program(g, core, T, topo):
     g.scalar.dma_start(idn, T.ed[0:128, :]).then_inc(S.er, 16)
 
     peers = [m for m in range(len(grp)) if m != mi]
-    g.wait_ge(S.ldx, 16)
     if first:
         g.wait_ge(S.ldw, 16)
-    sent = _send(g, topo, core, [cores[grp[m]] for m in peers], whole[mi], arr[mi], S.sent)
+    sent = 0
+    for b in blocks:
+        g.wait_ge(S["ldx%d" % b], 16)
+        sent += _send(g, topo, core, [cores[grp[m]] for m in peers], piece(mi, b), arr[mi][b], S.sent)
 
     def arrived1(m):
         return _engines(_mask(topo, cores[grp[m]], [cores[grp[o]] for o in range(len(grp)) if o != m]))
 
     late, early = peers[0], peers[1]
     te.wait_ge(S.er, 16)
-    te.wait_ge(S.ldx, 16)
-    for h in blocks:
-        te.matmul(sb[h], idn, blk(xin[mi], h), True, False)
-    te.wait_ge(arr[early], arrived1(early))
-    for h in blocks:
-        te.matmul(sb[h], idn, blk(xin[early], h), False, False)
-    te.wait_ge(arr[late], arrived1(late))
-    for h in blocks:
-        te.matmul(sb[h], idn, blk(xin[late], h), False, True).then_inc(S["s_%d" % h], 1)
-    v.wait_ge(S.zs, 1)
-    for h in blocks:
-        v.wait_ge(S["s_%d" % h], 1)
-        v.tensor_tensor(blk(T.t, h), sb[h], blk(T.zero, h), AluOpType.max).then_inc(S["r_%d" % h], 1)
+    for b in blocks:
+        te.wait_ge(S["ldx%d" % b], 16)
+        for h in subs(b):
+            te.matmul(sb[h], idn, xs(mi, h), True, False)
     if first:
         te.wait_ge(S.ldw, 16)
-    for h in blocks:
-        te.wait_ge(S["r_%d" % h], 1)
-        te.matmul(pp[h], wg, blk(T.t, h), True, True).then_inc(S["mm_%d" % h], 1)
-    for h in blocks:
-        v.wait_ge(S["mm_%d" % h], 1)
-        v.tensor_copy(blk(q[gi], h), pp[h]).then_inc(S["cp_%d" % h], 1)
-    for h in blocks:
-        te.matmul(sb[h], wg, blk(T.t, h), True, False)
+    v.wait_ge(S.zs, 1)
+    for b in blocks:
+        te.wait_ge(arr[early][b], arrived1(early))
+        for h in subs(b):
+            te.matmul(sb[h], idn, xs(early, h), False, False)
+        te.wait_ge(arr[late][b], arrived1(late))
+        for h in subs(b):
+            te.matmul(sb[h], idn, xs(late, h), False, True).then_inc(S["s_%d" % h], 1)
+        for h in subs(b):
+            v.wait_ge(S["s_%d" % h], 1)
+            v.tensor_tensor(sub(T.t, h), sb[h], sub(T.zero, h), AluOpType.max).then_inc(S["r_%d" % h], 1)
+        for h in subs(b):
+            te.wait_ge(S["r_%d" % h], 1)
+            te.matmul(pp[h], wg, sub(T.t, h), True, True).then_inc(S["mm_%d" % h], 1)
+        for h in subs(b):
+            v.wait_ge(S["mm_%d" % h], 1)
+            v.tensor_copy(sub(q[gi], h), pp[h]).then_inc(S["cp_%d" % h], 1)
+        for h in subs(b):
+            te.matmul(sb[h], wg, sub(T.t, h), True, False)
 
-    for h in blocks:
-        g.wait_ge(S["cp_%d" % h], 1)
-    sent += _send(g, topo, core, [cores[r] for r in plan[rank]], q[gi][:, :], par[gi], S.sent)
+    for b in blocks:
+        for h in subs(b):
+            g.wait_ge(S["cp_%d" % h], 1)
+        sent += _send(g, topo, core, [cores[r] for r in plan[rank]], blk(q[gi], b), par[gi][b], S.sent)
+
+    def server(k):
+        return [r for r in groups[k] if rank in plan[r]][0]
 
     def arrived2(k):
-        src = [r for r in groups[k] if rank in plan[r]][0]
+        src = server(k)
         return _engines(_mask(topo, cores[src], [cores[r] for r in plan[src]]))
 
-    ga, gb = [k for k in range(len(groups)) if k != gi]
-    te.wait_ge(par[ga], arrived2(ga))
-    for h in blocks:
-        te.matmul(sb[h], idn, blk(q[ga], h), False, True).then_inc(S["fa_%d" % h], 1)
-    v.wait_ge(par[gb], arrived2(gb))
-    for h in blocks:
-        v.wait_ge(S["fa_%d" % h], 1)
-        v.tensor_tensor(blk(T.yb, h), sb[h], blk(q[gb], h), AluOpType.add).then_inc(S["f2_%d" % h], 1)
-    for h in blocks:
-        g.sync.wait_ge(S["f2_%d" % h], 1)
-    g.sync.dma_start(T.y[:, :], T.yb[:, :]).then_inc(S.st, 16)
-    g.sync.wait_ge(S.st, 16)
+    def lateness(k):
+        return (0 if groups[k][0] == server(k) else 1, len(_links(topo, cores[server(k)], core)), k)
+
+    ga, gb = sorted([k for k in range(len(groups)) if k != gi], key=lateness)
+    for b in blocks:
+        te.wait_ge(par[ga][b], arrived2(ga))
+        for h in subs(b):
+            te.matmul(sb[h], idn, sub(q[ga], h), False, True).then_inc(S["fa_%d" % h], 1)
+        v.wait_ge(par[gb][b], arrived2(gb))
+        for h in subs(b):
+            v.wait_ge(S["fa_%d" % h], 1)
+            v.tensor_tensor(sub(T.yb, h), sb[h], sub(q[gb], h), AluOpType.add).then_inc(S["f2_%d" % h], 1)
+        qu = g.sync if b % 2 == 0 else g.scalar
+        for h in subs(b):
+            qu.wait_ge(S["f2_%d" % h], 1)
+        qu.dma_start(blk(T.y, b), blk(T.yb, b)).then_inc(S["st%d" % b], 16)
+        qu.wait_ge(S["st%d" % b], 16)
     g.wait_ge(S.sent, sent)

@@ -9,28 +9,36 @@ BW = F // RB
 SB = 2
 H = BW // SB
 NS = RB * SB
+CA = 32
+WCUT = [0, CA, K]
+WP = len(WCUT) - 1
 
 SCRATCH = {
-    "in0": ("sbuf", [128, K + F], "bfloat16"),
+    "in0": ("sbuf", [128, F], "bfloat16"),
     "in1": ("sbuf", [128, F], "bfloat16"),
     "in2": ("sbuf", [128, F], "bfloat16"),
+    "w0": ("sbuf", [128, K], "bfloat16"),
+    "w1": ("sbuf", [128, K], "bfloat16"),
+    "w2": ("sbuf", [128, K], "bfloat16"),
     "e": ("sbuf", [128, K + 1], "bfloat16"),
     "ed": ("dram", [K + 1, 128], "bfloat16"),
     "idn": ("sbuf", [128, K], "bfloat16"),
     "zero": ("sbuf", [128, F], "bfloat16"),
-    "t": ("sbuf", [128, F], "bfloat16"),
-    "q0": ("sbuf", [128, F], "bfloat16"),
-    "q1": ("sbuf", [128, F], "bfloat16"),
-    "q2": ("sbuf", [128, F], "bfloat16"),
+    "t0": ("sbuf", [128, F], "bfloat16"),
+    "t1": ("sbuf", [128, F], "bfloat16"),
+    "t2": ("sbuf", [128, F], "bfloat16"),
     "yb": ("sbuf", [128, F], "bfloat16"),
 }
-SEMAPHORES = ["ldw", "zs", "e1", "e2", "ew", "er", "sent"]
+SEMAPHORES = ["ldw", "wa0", "wa1", "wa2", "zs", "e1", "e2", "ew", "er", "sent"]
+for _p in range(WP):
+    SCRATCH["wd%d" % _p] = ("dram", [128, WCUT[_p + 1] - WCUT[_p]], "bfloat16")
+    SEMAPHORES += ["ldd%d" % _p, "wl%d" % _p]
 for _b in range(RB):
     SEMAPHORES += ["st%d" % _b, "ldx%d" % _b] + ["arr%d_%d" % (_m, _b) for _m in range(3)] + ["par%d_%d" % (_m, _b) for _m in range(3)]
 for _h in range(NS):
     SCRATCH["sb%d" % _h] = ("psum", [128, 512], "float32")
-    SCRATCH["pp%d" % _h] = ("psum", [128, 512], "float32")
-    SEMAPHORES += [n + str(_h) for n in ("s_", "r_", "mm_", "cp_", "fa_", "f2_")]
+    SCRATCH["yy%d" % _h] = ("psum", [128, 512], "float32")
+    SEMAPHORES += [n + str(_h) for n in ("s_", "r_", "fa_", "f2_")]
 
 
 def _place(topo, c):
@@ -81,6 +89,34 @@ def _round2_plan(topo, cores, groups):
     return plan
 
 
+def _w_plan(topo, cores, groups):
+    plan = []
+    for grp in groups:
+        src = cores[grp[0]]
+        helpers = [c for c in range(WORLD) if c not in cores and _place(topo, c) == _place(topo, src)]
+        dests = [r for r in range(len(cores)) if r != grp[0]]
+        can, reach, share, near = {}, {}, {}, {}
+        for r in dests:
+            can[r] = [h for h in helpers if topo.may_write(h, cores[r])]
+        for h in helpers:
+            reach[h] = len([r for r in dests if h in can[r]])
+            share[h] = []
+            near[h] = 1 if topo.die(h) == topo.die(src) else 0
+        for r in sorted(dests, key=lambda r: (len(can[r]), -len(_links(topo, src, cores[r])), r)):
+            h = min(can[r], key=lambda h: (len(share[h]) + near[h], near[h], reach[h], h))
+            share[h].append(r)
+        kept = {}
+        for h in helpers:
+            if share[h]:
+                kept[h] = share[h]
+        plan.append(kept)
+    return plan
+
+
+def _hand_order(share):
+    return sorted(share, key=lambda h: (-len(share[h]), h))
+
+
 def _mask(topo, src, dsts):
     m = topo.mask(src, dsts[0])
     for d in dsts[1:]:
@@ -92,22 +128,50 @@ def _engines(mask):
     return bin(mask).count("1")
 
 
-def _send(g, topo, core, dsts, ap, remote_sem, local_sem):
-    mask = _mask(topo, core, dsts)
+def _chip_mask(topo, src, helpers, away):
+    m = _mask(topo, src, helpers)
+    off = 0
+    for a in away:
+        off |= topo.mask(src, a)
+    spare = m & ~off
+    n = _engines(spare)
+    return spare if n > 0 and 128 % n == 0 else m
+
+
+def _send(g, topo, core, dsts, src_ap, dst_ap, remote_sem, local_sem, mask=None):
+    if mask is None:
+        mask = _mask(topo, core, dsts)
     ids = []
     for d in dsts:
         rid, pid = topo.addr(d, core)
         ids.append(DstId(rid=rid, pnc=pid))
     g.remote_dma_fused([RemoteDMATransfer(dst_ids=ids, dma_engine_mask=mask, remote_sem=remote_sem,
-                                          srcs=[ap], dsts=[ap for _ in dsts], alu_op=0)], local_sem=local_sem)
+                                          srcs=[src_ap], dsts=[dst_ap for _ in dsts], alu_op=0)], local_sem=local_sem)
     return _engines(mask)
 
 
 def rank_program(g, core, T, topo):
+    groups, cores, S = T.tables["GROUPS"], T.cores, T.sem
+    wplan = _w_plan(topo, cores, groups)
+    w = [T.w0, T.w1, T.w2]
+    wd = [T["wd%d" % p][:, :] for p in range(WP)]
+
+    def hand_mask(k):
+        src = cores[groups[k][0]]
+        return _chip_mask(topo, src, _hand_order(wplan[k]), [c for c in cores if c != src])
+
     rank = T.rank_of(core)
     if rank is None:
+        for k in range(len(groups)):
+            if core in wplan[k]:
+                n = 0
+                for p in range(WP):
+                    g.wait_ge(S["wl%d" % p], _engines(hand_mask(k)))
+                    n += _send(g, topo, core, [cores[r] for r in wplan[k][core]], wd[p], w[k][:, WCUT[p]:WCUT[p + 1]],
+                               S["wa%d" % k], S.sent)
+                g.wait_ge(S.sent, n)
         return
-    groups, cores, S = T.tables["GROUPS"], T.cores, T.sem
+
     gi = [k for k, grp in enumerate(groups) if rank in grp][0]
     grp = groups[gi]
     mi = grp.index(rank)
@@ -126,27 +190,19 @@ def rank_program(g, core, T, topo):
         return t[:, b * BW:(b + 1) * BW]
 
     slot = [T.in0, T.in1, T.in2]
-    off = [K, 0, 0]
-
-    def xs(m, h):
-        return slot[m][:, off[m] + h * H:off[m] + (h + 1) * H]
-
-    def piece(m, b):
-        lo = 0 if b == 0 else off[m] + b * BW
-        return slot[m][:, lo:off[m] + (b + 1) * BW]
-
-    wg = T.in0[:, 0:K]
-    q = [T.q0, T.q1, T.q2]
+    t = [T.t0, T.t1, T.t2]
     arr = [[S["arr%d_%d" % (m, b)] for b in blocks] for m in range(3)]
     par = [[S["par%d_%d" % (k, b)] for b in blocks] for k in range(3)]
     sb = [T["sb%d" % h][:, 0:H] for h in range(NS)]
-    pp = [T["pp%d" % h][:, 0:H] for h in range(NS)]
+    yy = [T["yy%d" % h][:, 0:H] for h in range(NS)]
     idn = T.idn[:, :]
 
     for b in blocks:
-        g.sync.dma_start(slot[mi][:, off[mi] + b * BW:off[mi] + (b + 1) * BW], blk(T.x, b)).then_inc(S["ldx%d" % b], 16)
+        g.sync.dma_start(blk(slot[mi], b), blk(T.x, b)).then_inc(S["ldx%d" % b], 16)
     if first:
-        g.scalar.dma_start(wg, T.w[:, :]).then_inc(S.ldw, 16)
+        for p in range(WP):
+            g.scalar.dma_start(wd[p], T.w[:, WCUT[p]:WCUT[p + 1]]).then_inc(S["ldd%d" % p], 16)
+        g.scalar.dma_start(w[gi][:, :], T.w[:, :]).then_inc(S.ldw, 16)
 
     v.memset(T.e[:, :], 0.0).then_inc(S.e1, 1)
     v.wait_ge(S.e1, 1)
@@ -158,48 +214,40 @@ def rank_program(g, core, T, topo):
     g.scalar.dma_start(idn, T.ed[0:128, :]).then_inc(S.er, 16)
 
     peers = [m for m in range(len(grp)) if m != mi]
-    if first:
-        g.wait_ge(S.ldw, 16)
     sent = 0
     for b in blocks:
         g.wait_ge(S["ldx%d" % b], 16)
-        sent += _send(g, topo, core, [cores[grp[m]] for m in peers], piece(mi, b), arr[mi][b], S.sent)
+        sent += _send(g, topo, core, [cores[grp[m]] for m in peers], blk(slot[mi], b), blk(slot[mi], b), arr[mi][b], S.sent)
+    if first:
+        for p in range(WP):
+            g.wait_ge(S["ldd%d" % p], 16)
+            sent += _send(g, topo, core, _hand_order(wplan[gi]), wd[p], wd[p], S["wl%d" % p], S.sent, hand_mask(gi))
 
     def arrived1(m):
         return _engines(_mask(topo, cores[grp[m]], [cores[grp[o]] for o in range(len(grp)) if o != m]))
 
-    late, early = peers[0], peers[1]
+    early, late = sorted(peers, key=lambda m: (len(_links(topo, cores[grp[m]], core)), m))
     te.wait_ge(S.er, 16)
     for b in blocks:
         te.wait_ge(S["ldx%d" % b], 16)
         for h in subs(b):
-            te.matmul(sb[h], idn, xs(mi, h), True, False)
-    if first:
-        te.wait_ge(S.ldw, 16)
+            te.matmul(sb[h], idn, sub(slot[mi], h), True, False)
     v.wait_ge(S.zs, 1)
     for b in blocks:
         te.wait_ge(arr[early][b], arrived1(early))
         for h in subs(b):
-            te.matmul(sb[h], idn, xs(early, h), False, False)
+            te.matmul(sb[h], idn, sub(slot[early], h), False, False)
         te.wait_ge(arr[late][b], arrived1(late))
         for h in subs(b):
-            te.matmul(sb[h], idn, xs(late, h), False, True).then_inc(S["s_%d" % h], 1)
+            te.matmul(sb[h], idn, sub(slot[late], h), False, True).then_inc(S["s_%d" % h], 1)
         for h in subs(b):
             v.wait_ge(S["s_%d" % h], 1)
-            v.tensor_tensor(sub(T.t, h), sb[h], sub(T.zero, h), AluOpType.max).then_inc(S["r_%d" % h], 1)
-        for h in subs(b):
-            te.wait_ge(S["r_%d" % h], 1)
-            te.matmul(pp[h], wg, sub(T.t, h), True, True).then_inc(S["mm_%d" % h], 1)
-        for h in subs(b):
-            v.wait_ge(S["mm_%d" % h], 1)
-            v.tensor_copy(sub(q[gi], h), pp[h]).then_inc(S["cp_%d" % h], 1)
-        for h in subs(b):
-            te.matmul(sb[h], wg, sub(T.t, h), True, False)
+            v.tensor_tensor(sub(t[gi], h), sb[h], sub(T.zero, h), AluOpType.max).then_inc(S["r_%d" % h], 1)
 
     for b in blocks:
         for h in subs(b):
-            g.wait_ge(S["cp_%d" % h], 1)
-        sent += _send(g, topo, core, [cores[r] for r in plan[rank]], blk(q[gi], b), par[gi][b], S.sent)
+            g.wait_ge(S["r_%d" % h], 1)
+        sent += _send(g, topo, core, [cores[r] for r in plan[rank]], blk(t[gi], b), blk(t[gi], b), par[gi][b], S.sent)
 
     def server(k):
         return [r for r in groups[k] if rank in plan[r]][0]
@@ -208,18 +256,47 @@ def rank_program(g, core, T, topo):
         src = server(k)
         return _engines(_mask(topo, cores[src], [cores[r] for r in plan[src]]))
 
-    def lateness(k):
-        return (0 if groups[k][0] == server(k) else 1, len(_links(topo, cores[server(k)], core)), k)
+    def helper(k):
+        return [c for c in wplan[k] if rank in wplan[k][c]][0]
 
-    ga, gb = sorted([k for k in range(len(groups)) if k != gi], key=lateness)
+    def wait_w(k):
+        if groups[k][0] == rank:
+            te.wait_ge(S.ldw, 16)
+        else:
+            te.wait_ge(S["wa%d" % k], WP * _engines(_mask(topo, helper(k), [cores[r] for r in wplan[k][helper(k)]])))
+
+    def w_late(k):
+        if groups[k][0] == rank:
+            return (0, 0, 0, k)
+        hc = helper(k)
+        return (1, len(wplan[k][hc]), len(_links(topo, hc, core)), k)
+
+    ga, gb = sorted([k for k in range(len(groups)) if k != gi], key=lambda k: (len(_links(topo, cores[server(k)], core)), k))
+    ops = []
+    for k in sorted(range(len(groups)), key=w_late):
+        ops += [(k, h) for h in (range(NS) if k == gi else subs(0))]
+    for b in blocks[1:]:
+        for k in (ga, gb):
+            ops += [(k, h) for h in subs(b)]
+    have_w, have_t = [], []
+    for n, (k, h) in enumerate(ops):
+        if k not in have_w:
+            have_w.append(k)
+            wait_w(k)
+        if k == gi:
+            te.wait_ge(S["r_%d" % h], 1)
+        elif (k, h // SB) not in have_t:
+            have_t.append((k, h // SB))
+            te.wait_ge(par[k][h // SB], arrived2(k))
+        start = h not in [o[1] for o in ops[:n]]
+        stop = h not in [o[1] for o in ops[n + 1:]]
+        mm = te.matmul(yy[h], w[k][:, :], sub(t[k], h), start, stop)
+        if stop:
+            mm.then_inc(S["fa_%d" % h], 1)
     for b in blocks:
-        te.wait_ge(par[ga][b], arrived2(ga))
-        for h in subs(b):
-            te.matmul(sb[h], idn, sub(q[ga], h), False, True).then_inc(S["fa_%d" % h], 1)
-        v.wait_ge(par[gb][b], arrived2(gb))
         for h in subs(b):
             v.wait_ge(S["fa_%d" % h], 1)
-            v.tensor_tensor(sub(T.yb, h), sb[h], sub(q[gb], h), AluOpType.add).then_inc(S["f2_%d" % h], 1)
+            v.tensor_copy(sub(T.yb, h), yy[h]).then_inc(S["f2_%d" % h], 1)
         qu = g.sync if b % 2 == 0 else g.scalar
         for h in subs(b):
             qu.wait_ge(S["f2_%d" % h], 1)

from concourse.bass import DstId, RemoteDMATransfer
from concourse.mybir import AluOpType

F = 256
K = 128
WORLD = 256
RB = 2
BW = F // RB
SB = 2
H = BW // SB
NS = RB * SB
CA = 32
WCUT = [0, CA, K]
WP = len(WCUT) - 1

SCRATCH = {
    "in0": ("sbuf", [128, F], "bfloat16"),
    "in1": ("sbuf", [128, F], "bfloat16"),
    "in2": ("sbuf", [128, F], "bfloat16"),
    "w0": ("sbuf", [128, K], "bfloat16"),
    "w1": ("sbuf", [128, K], "bfloat16"),
    "w2": ("sbuf", [128, K], "bfloat16"),
    "e": ("sbuf", [128, K + 1], "bfloat16"),
    "ed": ("dram", [K + 1, 128], "bfloat16"),
    "idn": ("sbuf", [128, K], "bfloat16"),
    "zero": ("sbuf", [128, F], "bfloat16"),
    "t0": ("sbuf", [128, F], "bfloat16"),
    "t1": ("sbuf", [128, F], "bfloat16"),
    "t2": ("sbuf", [128, F], "bfloat16"),
    "yb": ("sbuf", [128, F], "bfloat16"),
}
SEMAPHORES = ["ldw", "wa0", "wa1", "wa2", "zs", "e1", "e2", "ew", "er", "sent"]
for _p in range(WP):
    SCRATCH["wd%d" % _p] = ("dram", [128, WCUT[_p + 1] - WCUT[_p]], "bfloat16")
    SEMAPHORES += ["ldd%d" % _p, "wl%d" % _p]
for _b in range(RB):
    SEMAPHORES += ["st%d" % _b, "ldx%d" % _b] + ["arr%d_%d" % (_m, _b) for _m in range(3)] + ["par%d_%d" % (_m, _b) for _m in range(3)]
for _h in range(NS):
    SCRATCH["sb%d" % _h] = ("psum", [128, 512], "float32")
    SCRATCH["yy%d" % _h] = ("psum", [128, 512], "float32")
    SEMAPHORES += [n + str(_h) for n in ("s_", "r_", "fa_", "f2_")]


def _place(topo, c):
    return (topo.host(c), topo.chip(c))


def _links(topo, a, b):
    if _place(topo, a) == _place(topo, b):
        return []
    d = topo.die(a)
    if topo.mates(a, b):
        return [("mate", _place(topo, a), d)]
    if topo.same_plane(a, b):
        return [("out", _place(topo, a), d), ("in", _place(topo, b), d)]
    m = [c for c in range(WORLD) if topo.mates(a, c)][0]
    return [("mate", _place(topo, a), d), ("out", _place(topo, m), d), ("in", _place(topo, b), d)]


def _splits(items):
    out = []
    n = len(items)
    for a in range(n):
        for b in range(a + 1, n):
            rest = [items[k] for k in range(n) if k != a and k != b]
            for c in range(1, len(rest)):
                last = [rest[k] for k in range(1, len(rest)) if k != c]
                for pair2, pair3 in (([rest[0], rest[c]], last), (last, [rest[0], rest[c]])):
                    out.append([items[a], items[b]] + pair2 + pair3)
    return out


def _round2_plan(topo, cores, groups):
    load, plan = {}, {}
    for grp in groups:
        outs = [r for r in range(len(cores)) if r not in grp]
        best = None
        for p in _splits(outs):
            l = dict(load)
            for k, r in enumerate(p):
                for key in _links(topo, cores[grp[k // 2]], cores[r]):
                    l[key] = l.get(key, 0) + 1
            score = sum(v * v for v in l.values())
            if best is None or score < best[0]:
                best = (score, p, l)
        load = best[2]
        for k, r in enumerate(best[1]):
            plan.setdefault(grp[k // 2], []).append(r)
    return plan


def _w_plan(topo, cores, groups):
    plan = []
    for grp in groups:
        src = cores[grp[0]]
        helpers = [c for c in range(WORLD) if c not in cores and _place(topo, c) == _place(topo, src)]
        dests = [r for r in range(len(cores)) if r != grp[0]]
        can, reach, share, near = {}, {}, {}, {}
        for r in dests:
            can[r] = [h for h in helpers if topo.may_write(h, cores[r])]
        for h in helpers:
            reach[h] = len([r for r in dests if h in can[r]])
            share[h] = []
            near[h] = 1 if topo.die(h) == topo.die(src) else 0
        for r in sorted(dests, key=lambda r: (len(can[r]), -len(_links(topo, src, cores[r])), r)):
            h = min(can[r], key=lambda h: (len(share[h]) + near[h], near[h], reach[h], h))
            share[h].append(r)
        kept = {}
        for h in helpers:
            if share[h]:
                kept[h] = share[h]
        plan.append(kept)
    return plan


def _hand_order(share):
    return sorted(share, key=lambda h: (-len(share[h]), h))


def _mask(topo, src, dsts):
    m = topo.mask(src, dsts[0])
    for d in dsts[1:]:
        m &= topo.mask(src, d)
    return m


def _engines(mask):
    return bin(mask).count("1")


def _chip_mask(topo, src, helpers, away):
    m = _mask(topo, src, helpers)
    off = 0
    for a in away:
        off |= topo.mask(src, a)
    spare = m & ~off
    n = _engines(spare)
    return spare if n > 0 and 128 % n == 0 else m


def _send(g, topo, core, dsts, src_ap, dst_ap, remote_sem, local_sem, mask=None):
    if mask is None:
        mask = _mask(topo, core, dsts)
    ids = []
    for d in dsts:
        rid, pid = topo.addr(d, core)
        ids.append(DstId(rid=rid, pnc=pid))
    g.remote_dma_fused([RemoteDMATransfer(dst_ids=ids, dma_engine_mask=mask, remote_sem=remote_sem,
                                          srcs=[src_ap], dsts=[dst_ap for _ in dsts], alu_op=0)], local_sem=local_sem)
    return _engines(mask)


def rank_program(g, core, T, topo):
    groups, cores, S = T.tables["GROUPS"], T.cores, T.sem
    wplan = _w_plan(topo, cores, groups)
    w = [T.w0, T.w1, T.w2]
    wd = [T["wd%d" % p][:, :] for p in range(WP)]

    def hand_mask(k):
        src = cores[groups[k][0]]
        return _chip_mask(topo, src, _hand_order(wplan[k]), [c for c in cores if c != src])

    rank = T.rank_of(core)
    if rank is None:
        for k in range(len(groups)):
            if core in wplan[k]:
                n = 0
                for p in range(WP):
                    g.wait_ge(S["wl%d" % p], _engines(hand_mask(k)))
                    n += _send(g, topo, core, [cores[r] for r in wplan[k][core]], wd[p], w[k][:, WCUT[p]:WCUT[p + 1]],
                               S["wa%d" % k], S.sent)
                g.wait_ge(S.sent, n)
        return

    gi = [k for k, grp in enumerate(groups) if rank in grp][0]
    grp = groups[gi]
    mi = grp.index(rank)
    first = mi == 0
    plan = _round2_plan(topo, cores, groups)
    v, te = g.vector, g.tensor
    blocks = range(RB)

    def subs(b):
        return range(b * SB, (b + 1) * SB)

    def sub(t, h):
        return t[:, h * H:(h + 1) * H]

    def blk(t, b):
        return t[:, b * BW:(b + 1) * BW]

    slot = [T.in0, T.in1, T.in2]
    t = [T.t0, T.t1, T.t2]
    arr = [[S["arr%d_%d" % (m, b)] for b in blocks] for m in range(3)]
    par = [[S["par%d_%d" % (k, b)] for b in blocks] for k in range(3)]
    sb = [T["sb%d" % h][:, 0:H] for h in range(NS)]
    yy = [T["yy%d" % h][:, 0:H] for h in range(NS)]
    idn = T.idn[:, :]

    for b in blocks:
        g.sync.dma_start(blk(slot[mi], b), blk(T.x, b)).then_inc(S["ldx%d" % b], 16)
    if first:
        for p in range(WP):
            g.scalar.dma_start(wd[p], T.w[:, WCUT[p]:WCUT[p + 1]]).then_inc(S["ldd%d" % p], 16)
        g.scalar.dma_start(w[gi][:, :], T.w[:, :]).then_inc(S.ldw, 16)

    v.memset(T.e[:, :], 0.0).then_inc(S.e1, 1)
    v.wait_ge(S.e1, 1)
    v.memset(T.e[:, 0:1], 1.0).then_inc(S.e2, 1)
    v.memset(T.zero[:, :], 0.0).then_inc(S.zs, 1)
    g.scalar.wait_ge(S.e2, 1)
    g.scalar.dma_start(T.ed[:, :], T.e[:, :]).then_inc(S.ew, 16)
    g.scalar.wait_ge(S.ew, 16)
    g.scalar.dma_start(idn, T.ed[0:128, :]).then_inc(S.er, 16)

    peers = [m for m in range(len(grp)) if m != mi]
    sent = 0
    for b in blocks:
        g.wait_ge(S["ldx%d" % b], 16)
        sent += _send(g, topo, core, [cores[grp[m]] for m in peers], blk(slot[mi], b), blk(slot[mi], b), arr[mi][b], S.sent)
    if first:
        for p in range(WP):
            g.wait_ge(S["ldd%d" % p], 16)
            sent += _send(g, topo, core, _hand_order(wplan[gi]), wd[p], wd[p], S["wl%d" % p], S.sent, hand_mask(gi))

    def arrived1(m):
        return _engines(_mask(topo, cores[grp[m]], [cores[grp[o]] for o in range(len(grp)) if o != m]))

    early, late = sorted(peers, key=lambda m: (len(_links(topo, cores[grp[m]], core)), m))
    te.wait_ge(S.er, 16)
    for b in blocks:
        te.wait_ge(S["ldx%d" % b], 16)
        for h in subs(b):
            te.matmul(sb[h], idn, sub(slot[mi], h), True, False)
    v.wait_ge(S.zs, 1)
    for b in blocks:
        te.wait_ge(arr[early][b], arrived1(early))
        for h in subs(b):
            te.matmul(sb[h], idn, sub(slot[early], h), False, False)
        te.wait_ge(arr[late][b], arrived1(late))
        for h in subs(b):
            te.matmul(sb[h], idn, sub(slot[late], h), False, True).then_inc(S["s_%d" % h], 1)
        for h in subs(b):
            v.wait_ge(S["s_%d" % h], 1)
            v.tensor_tensor(sub(t[gi], h), sb[h], sub(T.zero, h), AluOpType.max).then_inc(S["r_%d" % h], 1)

    for b in blocks:
        for h in subs(b):
            g.wait_ge(S["r_%d" % h], 1)
        sent += _send(g, topo, core, [cores[r] for r in plan[rank]], blk(t[gi], b), blk(t[gi], b), par[gi][b], S.sent)

    def server(k):
        return [r for r in groups[k] if rank in plan[r]][0]

    def arrived2(k):
        src = server(k)
        return _engines(_mask(topo, cores[src], [cores[r] for r in plan[src]]))

    def helper(k):
        return [c for c in wplan[k] if rank in wplan[k][c]][0]

    def wait_w(k):
        if groups[k][0] == rank:
            te.wait_ge(S.ldw, 16)
        else:
            te.wait_ge(S["wa%d" % k], WP * _engines(_mask(topo, helper(k), [cores[r] for r in wplan[k][helper(k)]])))

    def w_late(k):
        if groups[k][0] == rank:
            return (0, 0, 0, k)
        hc = helper(k)
        return (1, len(wplan[k][hc]), len(_links(topo, hc, core)), k)

    ga, gb = sorted([k for k in range(len(groups)) if k != gi], key=lambda k: (len(_links(topo, cores[server(k)], core)), k))
    ops = []
    for k in sorted(range(len(groups)), key=w_late):
        ops += [(k, h) for h in (range(NS) if k == gi else subs(0))]
    for b in blocks[1:]:
        for k in (ga, gb):
            ops += [(k, h) for h in subs(b)]
    have_w, have_t = [], []
    for n, (k, h) in enumerate(ops):
        if k not in have_w:
            have_w.append(k)
            wait_w(k)
        if k == gi:
            te.wait_ge(S["r_%d" % h], 1)
        elif (k, h // SB) not in have_t:
            have_t.append((k, h // SB))
            te.wait_ge(par[k][h // SB], arrived2(k))
        start = h not in [o[1] for o in ops[:n]]
        stop = h not in [o[1] for o in ops[n + 1:]]
        mm = te.matmul(yy[h], w[k][:, :], sub(t[k], h), start, stop)
        if stop:
            mm.then_inc(S["fa_%d" % h], 1)
    for b in blocks:
        for h in subs(b):
            v.wait_ge(S["fa_%d" % h], 1)
            v.tensor_copy(sub(T.yb, h), yy[h]).then_inc(S["f2_%d" % h], 1)
        qu = g.sync if b % 2 == 0 else g.scalar
        for h in subs(b):
            qu.wait_ge(S["f2_%d" % h], 1)
        qu.dma_start(blk(T.y, b), blk(T.yb, b)).then_inc(S["st%d" % b], 16)
        qu.wait_ge(S["st%d" % b], 16)
    g.wait_ge(S.sent, sent)
